import numpy as np
import ml_dtypes


def mxq(x, axis, fmt="e4m3"):
    dtype, down = {"e4m3": (ml_dtypes.float8_e4m3fn, 7), "e5m2": (ml_dtypes.float8_e5m2, 14)}[fmt]
    v = np.moveaxis(np.asarray(x, np.float32).astype(ml_dtypes.bfloat16).astype(np.float64), axis, -1)
    blocks = v.reshape(v.shape[:-1] + (-1, 32))
    amax = np.abs(blocks).max(-1, keepdims=True)
    byte = np.maximum(np.where(amax > 0, np.frexp(amax)[1] - 1 + 127, 0) - down, 1)
    scale = np.exp2(byte - 127.0)
    codes = (blocks / scale).astype(np.float32).astype(dtype).astype(np.float64)
    return np.moveaxis((codes * scale).reshape(v.shape), -1, axis)


WIDE = False


def mx_kscale(k):
    if not WIDE:
        return np.ones(k)
    levels = np.array([10, -10, 5, -5, 0])
    if k % 512:
        return np.exp2(np.random.permutation(np.resize(levels, k // 32))).repeat(32)
    a = np.empty((k // 512, 16))
    for p in range(k // 512):
        a[p, :8] = np.random.permutation(np.resize(levels, 8))
        for g in range(8):
            far = levels[np.abs(levels - a[p, g]) >= 10]
            a[p, g + 8] = far[np.random.randint(len(far))]
    return np.exp2(a.ravel()).repeat(32)


BF16 = ml_dtypes.bfloat16


def bf(x):
    return np.asarray(x, np.float32).astype(BF16)


def f64(x):
    return np.asarray(x).astype(np.float64)


E2M1 = np.array([0.0, 0.5, 1.0, 1.5, 2.0, 3.0, 4.0, 6.0, -0.0, -0.5, -1.0, -1.5, -2.0, -3.0, -4.0, -6.0])


def pack_weight(w, fmt):
    k, n = w.shape
    w = f64(bf(w)).reshape(k // 32, 32, n)
    amax = np.abs(w).max(1)
    if fmt == "e4m3":
        byte = np.frexp(amax)[1] - 1 + 127 - 7
    else:
        mant, ex = np.frexp(amax / 6.0)
        byte = np.where(mant > 0.5, ex, ex - 1) + 127
    byte = np.clip(np.where(amax > 0, byte, 1), 1, 254)
    scaled = (w * np.exp2(127.0 - byte)[:, None, :]).reshape(k, n).astype(np.float32)
    by_word = np.ascontiguousarray(scaled.reshape(k // 512, 128, 4, n).transpose(0, 1, 3, 2))
    if fmt == "e4m3":
        words = by_word.astype(ml_dtypes.float8_e4m3fn).view(np.uint8)
    else:
        c = by_word.astype(ml_dtypes.float4_e2m1fn).view(np.uint8) & 0xF
        words = c[..., 0::2] | (c[..., 1::2] << 4)
    return np.ascontiguousarray(words), np.ascontiguousarray(byte.astype(np.uint8).reshape(k // 512, 16, n))


def unpack_weight(words, scales, fmt):
    g, p, n, _ = words.shape
    if fmt == "e4m3":
        vals = np.ascontiguousarray(words).view(ml_dtypes.float8_e4m3fn).astype(np.float64)
    else:
        nib = np.empty((g, p, n, 4), np.uint8)
        nib[..., 0::2] = words & 0xF
        nib[..., 1::2] = words >> 4
        vals = E2M1[nib]
    vals = vals * np.repeat(np.exp2(scales.astype(np.float64) - 127.0), 8, axis=1)[..., None]
    return vals.transpose(0, 1, 3, 2).reshape(g * 512, n)
def pack4(w):
    words, scales = pack_weight(w, "e2m1")
    return words.reshape(words.shape[0], 128, -1), scales


def unpack4(words, scales):
    return unpack_weight(words.reshape(words.shape[0], 128, -1, 2), scales, "e2m1")


T, D, J, V = 512, 1536, 1024, 2048


def setup_inputs():
    s = mx_kscale(D)
    v = mx_kscale(V)
    t = mx_kscale(J)
    chosen = np.exp(2.0 * np.random.standard_normal((J, V)))
    rejected = np.exp(2.0 * np.random.standard_normal((J, V)))
    chosen = chosen / chosen.sum(axis=1, keepdims=True)
    rejected = rejected / rejected.sum(axis=1, keepdims=True)
    ut_words, ut_scales = pack4(np.random.standard_normal((V, D)) / v[:, None])
    return {"h": bf(np.random.standard_normal((T, D)) * s),
            "r": bf(2.0 * np.random.standard_normal((D, J)) / np.sqrt(D) / s[:, None]),
            "beta": bf((1.0 + 0.1 * np.random.standard_normal(J)) * t),
            "p_chosen": bf(chosen * v / t[:, None]),
            "p_rejected": bf(rejected * v / t[:, None]),
            "ut_words": ut_words, "ut_scales": ut_scales}


def reference(h, r, beta, p_chosen, p_rejected, ut_words, ut_scales):
    m = mxq(f64(h), 1, "e4m3") @ mxq(f64(r), 0, "e4m3")
    w = f64(beta) / (1.0 + np.exp(-m))
    diff = f64(p_chosen) - f64(p_rejected)
    b = mxq(diff, 1, "e4m3") @ unpack4(ut_words, ut_scales)
    return mxq(w, 1, "e4m3") @ mxq(b, 0, "e4m3")

@@ -1,0 +1,449 @@
+from contextlib import ExitStack
+
+import concourse.mybir as mybir
+from concourse.masks import make_identity
+
+T, D, J, V = 512, 1536, 1024, 2048
+P = 128
+FLOPS = 2 * (T * D * J + J * V * D + T * J * D)
+
+F32 = mybir.dt.float32
+BF16 = mybir.dt.bfloat16
+I32 = mybir.dt.int32
+U32 = mybir.dt.uint32
+U8 = mybir.dt.uint8
+FP8X4 = mybir.dt.float8_e4m3fn_x4
+FP4X4 = mybir.dt.float4_e2m1fn_x4
+ACT = mybir.ActivationFunctionType
+ALU = mybir.AluOpType
+
+NV = V // 512
+ND = D // 512
+NJ = J // 512
+NT = T // P
+TPB = 2
+
+
+def tile_dpo_like_hidden_step_s11_kernel(tc, h, r, beta, p_chosen, p_rejected, ut_words, ut_scales, out):
+    nc = tc.nc
+    with ExitStack() as ctx:
+        keep = ctx.enter_context(tc.tile_pool(name="keep", bufs=1))
+        work = ctx.enter_context(tc.tile_pool(name="work", bufs=2))
+        tp_pool = ctx.enter_context(tc.psum_pool(name="tp_pool", bufs=TPB))
+        acc_pool = ctx.enter_context(tc.psum_pool(name="acc_pool", bufs=8 - TPB))
+        ctx.enter_context(tc.manual_schedule())
+
+        ident = keep.tile([P, P], F32, name="ident")
+        warm = keep.tile([P, 1], F32, name="warm")
+        beta_bf = keep.tile([P, NJ, 4], BF16, name="beta_bf")
+        beta_f = keep.tile([P, NJ, 4], F32, name="beta_f")
+        usc = keep.tile([P, NV, D], U8, name="usc", align_bytes=64)
+        ut0 = keep.tile([P, NV, 1024], U8, name="ut0", align_bytes=64)
+        ut12 = keep.tile([P, NV, 2048], U8, name="ut12", align_bytes=64)
+        hraw = keep.tile([P, NT, D], BF16, name="hraw", align_bytes=64)
+        hcodes, hscales, rcodes, rscales = [], [], [], []
+        for k in range(ND):
+            t1 = keep.tile([P, T], U32, name="hc%d" % k, align_bytes=64)
+            t2 = keep.tile([P, T], U8, name="hs%d" % k, align_bytes=64)
+            t3 = keep.tile([P, J], U32, name="rc%d" % k, align_bytes=64)
+            t4 = keep.tile([P, J], U8, name="rs%d" % k, align_bytes=64)
+            hcodes.append(t1)
+            hscales.append(t2)
+            rcodes.append(t3)
+            rscales.append(t4)
+        acodes, ascales, bcodes, bscales, sig = [], [], [], [], []
+        braw = keep.tile([P, 4, D], BF16, name="braw", align_bytes=64)
+        for g in range(NJ):
+            t1 = keep.tile([P, T], U32, name="ac%d" % g, align_bytes=64)
+            t2 = keep.tile([P, T], U8, name="as%d" % g, align_bytes=64)
+            t3 = keep.tile([P, D], U32, name="bc%d" % g, align_bytes=64)
+            t4 = keep.tile([P, D], U8, name="bs%d" % g, align_bytes=64)
+            t6 = keep.tile([P, 4, T], F32, name="sig%d" % g, align_bytes=64)
+            acodes.append(t1)
+            ascales.append(t2)
+            bcodes.append(t3)
+            bscales.append(t4)
+            sig.append(t6)
+
+        pc, pr, rraw = {}, {}, {}
+
+        def load_p(q, pieces=1):
+            g, t = q // 4, q % 4
+            a = work.tile([P, V], BF16, name="pc", tag="pc", bufs=4, align_bytes=64)
+            b = work.tile([P, V], BF16, name="pr", tag="pr", bufs=4, align_bytes=64)
+            w = V // pieces
+            rows = slice(g * 512, (g + 1) * 512)
+            src_a = p_chosen[rows, :].rearrange("(m t) v -> m t v", t=4)
+            src_b = p_rejected[rows, :].rearrange("(m t) v -> m t v", t=4)
+            for i in range(pieces):
+                cols = slice(i * w, (i + 1) * w)
+                nc.sync.dma_start(out=a[:, cols], in_=src_a[:, t, cols])
+                nc.sync.dma_start(out=b[:, cols], in_=src_b[:, t, cols])
+            pc[q], pr[q] = a, b
+
+        def load_ut(dst, lo):
+            nc.sync.dma_start(
+                out=dst[:].bitcast(I32),
+                in_=ut_words[:, :, lo : lo + dst.shape[2]].rearrange("g p c -> p g c").bitcast(I32),
+            )
+
+        def ut_cols(v, lo, w):
+            tile, at = (ut0, lo) if lo < 512 else (ut12, lo - 512)
+            return tile[:, v, 2 * at : 2 * (at + w)].bitcast(FP4X4)
+
+        def load_r(k):
+            x = work.tile([P, 4, J], BF16, name="rraw", tag="rraw", bufs=3, align_bytes=64)
+            nc.sync.dma_start(out=x[:], in_=r[k * 512 : (k + 1) * 512, :].rearrange("(p j) c -> p j c", j=4))
+            rraw[k] = x
+
+        diff, ct, cc, cs = {}, {}, {}, {}
+
+        def sub(q, pieces=1):
+            x = work.tile([P, 2, V // 4, 2], BF16, name="diff", tag="diff", bufs=2, align_bytes=64)
+            w = V // pieces
+            for i in range(pieces):
+                cols = slice(i * w, (i + 1) * w)
+                nc.vector.tensor_tensor(
+                    out=x[:, :, i * w // 4 : (i + 1) * w // 4, :],
+                    in0=pc[q][:, cols].rearrange("p (w u e) -> p u w e", u=2, e=2),
+                    in1=pr[q][:, cols].rearrange("p (w u e) -> p u w e", u=2, e=2),
+                    op=ALU.subtract,
+                )
+            diff[q] = x
+
+        bank = {}
+
+        def tr(q, b):
+            words = diff[q][:].rearrange("p u w e -> p (u w e)").bitcast(F32)
+            x = tp_pool.tile([P, 2, 2, P], F32, name="tp", tag="tp")
+            for a in range(2):
+                for u in range(2):
+                    lo = u * 512 + (2 * b + a) * P
+                    nc.tensor.transpose(x[:, a, u, :], words[:, lo : lo + P], ident[:])
+            bank[q, b] = x
+
+        def cp(q, b, eng):
+            if b == 0:
+                x = work.tile([P, NV, P, 4], BF16, name="ct", tag="ct", bufs=2, align_bytes=64)
+                ct[q] = x
+            dst = ct[q][:, 2 * b : 2 * b + 2, :, :].rearrange("p a r j -> p (a r j)").bitcast(F32)
+            move(eng, dst.rearrange("p (a r u) -> p a r u", a=2, u=2), bank[q, b][:].rearrange("p a u r -> p a r u"))
+
+        def move(eng, dst, src):
+            if eng == "s":
+                nc.scalar.copy(out=dst, in_=src)
+            else:
+                nc.vector.tensor_copy(out=dst, in_=src)
+
+        def quant_c(q, half=None):
+            if half in (None, 0):
+                x = work.tile([P, NV * P], U32, name="cc", tag="cc", bufs=6, align_bytes=64)
+                y = work.tile([P, NV * P], U8, name="cs", tag="cs", bufs=6, align_bytes=64)
+                cc[q], cs[q] = x, y
+            flat = ct[q][:].rearrange("p a r j -> p (a r j)")
+            lo, hi = (0, 512) if half is None else (256 * half, 256 * half + 256)
+            nc.vector.quantize_mx(
+                out=cc[q][:, lo:hi].bitcast(FP8X4), scales=cs[q][:, lo:hi], in_=flat[:, 4 * lo : 4 * hi]
+            )
+
+        bacc = {}
+
+        def mm_b(q, n):
+            x = acc_pool.tile([P, 512], F32, name="acc", tag="acc")
+            for v in range(NV):
+                nc.tensor.matmul_mx(
+                    out=x[:],
+                    lhsT=cc[q][:, v * P : (v + 1) * P].bitcast(FP8X4),
+                    lhsT_scale=cs[q][:, v * P : (v + 1) * P],
+                    rhs=ut_cols(v, n * 512, 512),
+                    rhs_scale=usc[:, v, n * 512 : (n + 1) * 512],
+                    start=(v == 0),
+                    stop=(v == NV - 1),
+                )
+            bacc[q, n] = x
+
+        def ev_b(q, n, eng):
+            move(eng, braw[:, q % 4, n * 512 : (n + 1) * 512], bacc[q, n][:])
+
+        def grp_tile():
+            x = work.tile([P, 512, 4], BF16, name="grp", tag="grp", bufs=6, align_bytes=64)
+            return x
+
+        gb = {}
+
+        def inter_b(g, n, eng):
+            x = grp_tile()
+            move(eng, x[:], braw[:, :, n * 512 : (n + 1) * 512].rearrange("p t n -> p n t"))
+            gb[g, n] = x
+
+        def quant_b(g, n):
+            cols = slice(n * 512, (n + 1) * 512)
+            nc.vector.quantize_mx(
+                out=bcodes[g][:, cols].bitcast(FP8X4), scales=bscales[g][:, cols],
+                in_=gb[g, n][:].rearrange("p c j -> p (c j)"),
+            )
+
+        def mm_u(u, ts):
+            if ts[0] == 0:
+                x = acc_pool.tile([P, 4, P], F32, name="acc", tag="acc")
+                bacc["u", u] = x
+            for t in ts:
+                for v in range(NV):
+                    nc.tensor.matmul_mx(
+                        out=bacc["u", u][:, t, :],
+                        lhsT=cc[4 + t][:, v * P : (v + 1) * P].bitcast(FP8X4),
+                        lhsT_scale=cs[4 + t][:, v * P : (v + 1) * P],
+                        rhs=ut_cols(v, u * P, P),
+                        rhs_scale=usc[:, v, u * P : (u + 1) * P],
+                        start=(v == 0),
+                        stop=(v == NV - 1),
+                    )
+
+        def ev_u(u, eng):
+            if u % 4 == 0:
+                x = grp_tile()
+                gb[1, u // 4] = x
+            c = u % 4
+            move(eng, gb[1, u // 4][:, c * P : (c + 1) * P, :], bacc["u", u][:].rearrange("p t n -> p n t"))
+
+        def quant_u(u):
+            cols = slice(u * P, (u + 1) * P)
+            c = u % 4
+            nc.vector.quantize_mx(
+                out=bcodes[1][:, cols].bitcast(FP8X4), scales=bscales[1][:, cols],
+                in_=gb[1, u // 4][:, c * P : (c + 1) * P, :].rearrange("p c j -> p (c j)"),
+            )
+
+        gr = {}
+
+        def inter_r(k, g, eng):
+            x = grp_tile()
+            move(
+                eng,
+                x[:].rearrange("p (t m) j -> p t m j", t=4),
+                rraw[k][:, :, g * 512 : (g + 1) * 512].rearrange("p j (m t) -> p t m j", t=4),
+            )
+            gr[k, g] = x
+
+        def quant_r(k, g):
+            cols = slice(g * 512, (g + 1) * 512)
+            nc.vector.quantize_mx(
+                out=rcodes[k][:, cols].bitcast(FP8X4), scales=rscales[k][:, cols],
+                in_=gr[k, g][:].rearrange("p c j -> p (c j)"),
+            )
+
+        gh, hbank = {}, {}
+
+        def tr_h(k):
+            for b in range(2):
+                x = tp_pool.tile([P, 2, 2, P], F32, name="tp", tag="tp")
+                for a in range(2):
+                    words = hraw[:, 2 * b + a, :].bitcast(F32)
+                    for u in range(2):
+                        nc.tensor.transpose(x[:, a, u, :], words[:, 256 * k + u : 256 * (k + 1) : 2], ident[:])
+                hbank[k, b] = x
+
+        def cp_h(k, b, eng):
+            if b == 0:
+                x = grp_tile()
+                gh[k] = x
+            dst = gh[k][:, 256 * b : 256 * b + 256, :].rearrange("p c j -> p (c j)").bitcast(F32)
+            move(eng, dst.rearrange("p (a r u) -> p a r u", a=2, u=2), hbank[k, b][:].rearrange("p a u r -> p a r u"))
+
+        def quant_h(k):
+            nc.vector.quantize_mx(
+                out=hcodes[k][:].bitcast(FP8X4), scales=hscales[k][:], in_=gh[k][:].rearrange("p c j -> p (c j)")
+            )
+
+        def mm_m(g, t):
+            x = acc_pool.tile([P, 512], F32, name="acc", tag="acc")
+            cols = slice(g * 512 + t * P, g * 512 + (t + 1) * P)
+            for k in range(ND):
+                nc.tensor.matmul_mx(
+                    out=x[:],
+                    lhsT=rcodes[k][:, cols].bitcast(FP8X4),
+                    lhsT_scale=rscales[k][:, cols],
+                    rhs=hcodes[k][:].bitcast(FP8X4),
+                    rhs_scale=hscales[k][:],
+                    start=(k == 0),
+                    stop=(k == ND - 1),
+                )
+            nc.scalar.activation(out=sig[g][:, t, :], in_=x[:], func=ACT.Sigmoid)
+
+        ga = {}
+
+        def mul_a(g):
+            x = grp_tile()
+            nc.vector.tensor_tensor(
+                out=x[:],
+                in0=sig[g][:].rearrange("p t n -> p n t"),
+                in1=beta_f[:, g : g + 1, :].to_broadcast([P, T, 4]),
+                op=ALU.mult,
+            )
+            ga[g] = x
+
+        def quant_a(g):
+            nc.vector.quantize_mx(
+                out=acodes[g][:].bitcast(FP8X4), scales=ascales[g][:], in_=ga[g][:].rearrange("p c j -> p (c j)")
+            )
+
+        oacc = {}
+
+        def mm_o(i, c0, w, g, pool=None):
+            if g == 0:
+                if pool == "tp":
+                    x = tp_pool.tile([P, 512], F32, name="tp", tag="tp")
+                else:
+                    x = acc_pool.tile([P, 512], F32, name="acc", tag="acc")
+                oacc[i, c0] = x
+            rows, cols = slice(i * P, (i + 1) * P), slice(c0, c0 + w)
+            nc.tensor.matmul_mx(
+                out=oacc[i, c0][:, 0:w],
+                lhsT=acodes[g][:, rows].bitcast(FP8X4),
+                lhsT_scale=ascales[g][:, rows],
+                rhs=bcodes[g][:, cols].bitcast(FP8X4),
+                rhs_scale=bscales[g][:, cols],
+                start=(g == 0),
+                stop=(g == NJ - 1),
+            )
+
+        def ev_o(i, c0, w, eng):
+            if w == 512:
+                x = work.tile([P, 512], F32, name="osb", tag="osb", bufs=6, align_bytes=64)
+            else:
+                x = work.tile([P, 256], F32, name="osh", tag="osh", bufs=8, align_bytes=64)
+            move(eng, x[:, 0:w], oacc[i, c0][:, 0:w])
+            nc.sync.dma_start(out=out[i * P : (i + 1) * P, c0 : c0 + w], in_=x[:, 0:w])
+
+        nc.vector.memset(usc[:].bitcast(I32), 0)
+        nc.gpsimd.memset(warm[:], 0.0)
+        nc.scalar.activation(out=warm[:], in_=warm[:], func=ACT.Sigmoid)
+        make_identity(nc, ident[:])
+        load_p(0, 2)
+        for rr in range(4):
+            nc.scalar.dma_start(
+                out=usc[rr:P:32, :, :].bitcast(I32),
+                in_=ut_scales[:, rr:16:4, :].rearrange("g q n -> q g n").bitcast(I32),
+            )
+        load_ut(ut0, 0)
+        load_p(1, 2)
+        load_ut(ut12, 1024)
+        load_p(2)
+        load_r(0)
+        load_p(3)
+        nc.sync.dma_start(out=hraw[:], in_=h.rearrange("(i p) k -> p i k", p=P))
+        load_r(1)
+        load_r(2)
+        nc.gpsimd.dma_start(out=beta_bf[:], in_=beta.rearrange("(g p t) -> p g t", g=NJ, t=4))
+
+        def run_c(q, half=False):
+            for b in range(2):
+                tr(q, b)
+                cp(q, b, "s")
+                if half:
+                    quant_c(q, b)
+            if not half:
+                quant_c(q)
+
+        def mmev(q, n, eng="s"):
+            mm_b(q, n)
+            ev_b(q, n, eng)
+
+        def run_h(k):
+            tr_h(k)
+            cp_h(k, 0, "s")
+            cp_h(k, 1, "s")
+
+        def r_v(k, g):
+            inter_r(k, g, "v")
+
+        sub(0, 2)
+        load_p(4)
+        run_c(0, True)
+        sub(1, 2)
+        load_p(5)
+        mmev(0, 0)
+        run_c(1, True)
+        mmev(1, 0)
+        mmev(0, 1)
+        mmev(0, 2)
+        sub(2)
+        load_p(6)
+        mmev(1, 1)
+        run_c(2, True)
+        mmev(1, 2)
+        inter_r(0, 0, "v")
+        sub(3)
+        quant_r(0, 0)
+        load_p(7)
+        mmev(2, 0)
+        mmev(2, 1)
+        run_c(3, True)
+        nc.vector.tensor_copy(out=beta_f[:], in_=beta_bf[:])
+        inter_r(0, 1, "v")
+        mmev(2, 2)
+        run_h(0)
+        quant_r(0, 1)
+        mmev(3, 0)
+        quant_h(0)
+        inter_r(1, 0, "v")
+        run_h(1)
+        quant_r(1, 0)
+        mmev(3, 1)
+        quant_h(1)
+        inter_r(2, 0, "v")
+        run_h(2)
+        mmev(3, 2)
+        quant_h(2)
+        quant_r(2, 0)
+        sub(4)
+        inter_r(1, 1, "s")
+        inter_r(2, 1, "v")
+        sub(5)
+        quant_r(1, 1)
+        quant_r(2, 1)
+        for t in range(4):
+            mm_m(0, t)
+        for t in range(4):
+            run_c(4 + t)
+            mm_m(1, t)
+            if t < 2:
+                sub(6 + t)
+            if t == 2:
+                mul_a(0)
+        quant_a(0)
+        for u in range(3):
+            mm_u(u, [0, 1, 2])
+        mul_a(1)
+        for u in range(3):
+            mm_u(u, [3])
+            ev_u(u, "s")
+            quant_u(u)
+        quant_a(1)
+        for n in range(ND):
+            inter_b(0, n, "v")
+            u = 3 + n
+            mm_u(u, [0, 1, 2, 3])
+            ev_u(u, "s")
+            quant_u(u)
+            quant_b(0, n)
+
+        def out_chunk(c0, w, between=None):
+            for i in range(NT):
+                mm_o(i, c0, w, 0, "tp" if i < 2 else None)
+            for i in range(NT):
+                mm_o(i, c0, w, 1)
+                ev_o(i, c0, w, "s" if i % 2 == 0 else "v")
+
+        out_chunk(0, 512)
+        for u in range(6, 10):
+            mm_u(u, [0, 1, 2, 3])
+            ev_u(u, "s")
+            quant_u(u)
+        out_chunk(512, 512)
+        for u in range(10, 12):
+            mm_u(u, [0, 1, 2, 3])
+            ev_u(u, "s")
+            quant_u(u)
+        out_chunk(1024, 256)
+        out_chunk(1280, 256)

@@ -21,7 +21,7 @@ NV = V // 512
 ND = D // 512
 NJ = J // 512
 NT = T // P
-TPB = 2
+TPB = 3
 
 
 def tile_dpo_like_hidden_step_s11_kernel(tc, h, r, beta, p_chosen, p_rejected, ut_words, ut_scales, out):
@@ -53,6 +53,7 @@ def tile_dpo_like_hidden_step_s11_kernel(tc, h, r, beta, p_chosen, p_rejected, u
             rscales.append(t4)
         acodes, ascales, bcodes, bscales, sig = [], [], [], [], []
         braw = keep.tile([P, 4, D], BF16, name="braw", align_bytes=64)
+        braw1 = keep.tile([P, 4, 1024], BF16, name="braw1", align_bytes=64)
         for g in range(NJ):
             t1 = keep.tile([P, T], U32, name="ac%d" % g, align_bytes=64)
             t2 = keep.tile([P, T], U8, name="as%d" % g, align_bytes=64)
@@ -67,19 +68,18 @@ def tile_dpo_like_hidden_step_s11_kernel(tc, h, r, beta, p_chosen, p_rejected, u
 
         pc, pr, rraw = {}, {}, {}
 
-        def load_p(q, pieces=1):
+        def load_p(q, half=None):
             g, t = q // 4, q % 4
-            a = work.tile([P, V], BF16, name="pc", tag="pc", bufs=4, align_bytes=64)
-            b = work.tile([P, V], BF16, name="pr", tag="pr", bufs=4, align_bytes=64)
-            w = V // pieces
+            if q not in pc:
+                a = work.tile([P, V], BF16, name="pc", tag="pc", bufs=4, align_bytes=64)
+                b = work.tile([P, V], BF16, name="pr", tag="pr", bufs=4, align_bytes=64)
+                pc[q], pr[q] = a, b
+            cols = slice(0, V) if half is None else slice(half * V // 2, (half + 1) * V // 2)
             rows = slice(g * 512, (g + 1) * 512)
             src_a = p_chosen[rows, :].rearrange("(m t) v -> m t v", t=4)
             src_b = p_rejected[rows, :].rearrange("(m t) v -> m t v", t=4)
-            for i in range(pieces):
-                cols = slice(i * w, (i + 1) * w)
-                nc.sync.dma_start(out=a[:, cols], in_=src_a[:, t, cols])
-                nc.sync.dma_start(out=b[:, cols], in_=src_b[:, t, cols])
-            pc[q], pr[q] = a, b
+            nc.sync.dma_start(out=pc[q][:, cols], in_=src_a[:, t, cols])
+            nc.sync.dma_start(out=pr[q][:, cols], in_=src_b[:, t, cols])
 
         def load_ut(dst, lo):
             nc.sync.dma_start(
@@ -92,24 +92,23 @@ def tile_dpo_like_hidden_step_s11_kernel(tc, h, r, beta, p_chosen, p_rejected, u
             return tile[:, v, 2 * at : 2 * (at + w)].bitcast(FP4X4)
 
         def load_r(k):
-            x = work.tile([P, 4, J], BF16, name="rraw", tag="rraw", bufs=3, align_bytes=64)
+            x = work.tile([P, 4, J], BF16, name="rraw", tag="rraw", bufs=2, align_bytes=64)
             nc.sync.dma_start(out=x[:], in_=r[k * 512 : (k + 1) * 512, :].rearrange("(p j) c -> p j c", j=4))
             rraw[k] = x
 
         diff, ct, cc, cs = {}, {}, {}, {}
 
-        def sub(q, pieces=1):
-            x = work.tile([P, 2, V // 4, 2], BF16, name="diff", tag="diff", bufs=2, align_bytes=64)
-            w = V // pieces
-            for i in range(pieces):
-                cols = slice(i * w, (i + 1) * w)
-                nc.vector.tensor_tensor(
-                    out=x[:, :, i * w // 4 : (i + 1) * w // 4, :],
-                    in0=pc[q][:, cols].rearrange("p (w u e) -> p u w e", u=2, e=2),
-                    in1=pr[q][:, cols].rearrange("p (w u e) -> p u w e", u=2, e=2),
-                    op=ALU.subtract,
-                )
-            diff[q] = x
+        def sub(q, half=None):
+            if q not in diff:
+                x = work.tile([P, 2, V // 4, 2], BF16, name="diff", tag="diff", bufs=2, align_bytes=64)
+                diff[q] = x
+            lo, hi = (0, V) if half is None else (half * V // 2, (half + 1) * V // 2)
+            nc.vector.tensor_tensor(
+                out=diff[q][:, :, lo // 4 : hi // 4, :],
+                in0=pc[q][:, lo:hi].rearrange("p (w u e) -> p u w e", u=2, e=2),
+                in1=pr[q][:, lo:hi].rearrange("p (w u e) -> p u w e", u=2, e=2),
+                op=ALU.subtract,
+            )
 
         bank = {}
 
@@ -123,7 +122,7 @@ def tile_dpo_like_hidden_step_s11_kernel(tc, h, r, beta, p_chosen, p_rejected, u
             bank[q, b] = x
 
         def cp(q, b, eng):
-            if b == 0:
+            if q not in ct:
                 x = work.tile([P, NV, P, 4], BF16, name="ct", tag="ct", bufs=2, align_bytes=64)
                 ct[q] = x
             dst = ct[q][:, 2 * b : 2 * b + 2, :, :].rearrange("p a r j -> p (a r j)").bitcast(F32)
@@ -136,7 +135,7 @@ def tile_dpo_like_hidden_step_s11_kernel(tc, h, r, beta, p_chosen, p_rejected, u
                 nc.vector.tensor_copy(out=dst, in_=src)
 
         def quant_c(q, half=None):
-            if half in (None, 0):
+            if q not in cc:
                 x = work.tile([P, NV * P], U32, name="cc", tag="cc", bufs=6, align_bytes=64)
                 y = work.tile([P, NV * P], U8, name="cs", tag="cs", bufs=6, align_bytes=64)
                 cc[q], cs[q] = x, y
@@ -163,7 +162,8 @@ def tile_dpo_like_hidden_step_s11_kernel(tc, h, r, beta, p_chosen, p_rejected, u
             bacc[q, n] = x
 
         def ev_b(q, n, eng):
-            move(eng, braw[:, q % 4, n * 512 : (n + 1) * 512], bacc[q, n][:])
+            dst = braw if q < 4 else braw1
+            move(eng, dst[:, q % 4, n * 512 : (n + 1) * 512], bacc[q, n][:])
 
         def grp_tile():
             x = work.tile([P, 512, 4], BF16, name="grp", tag="grp", bufs=6, align_bytes=64)
@@ -173,7 +173,8 @@ def tile_dpo_like_hidden_step_s11_kernel(tc, h, r, beta, p_chosen, p_rejected, u
 
         def inter_b(g, n, eng):
             x = grp_tile()
-            move(eng, x[:], braw[:, :, n * 512 : (n + 1) * 512].rearrange("p t n -> p n t"))
+            src = braw if g == 0 else braw1
+            move(eng, x[:], src[:, :, n * 512 : (n + 1) * 512].rearrange("p t n -> p n t"))
             gb[g, n] = x
 
         def quant_b(g, n):
@@ -184,7 +185,7 @@ def tile_dpo_like_hidden_step_s11_kernel(tc, h, r, beta, p_chosen, p_rejected, u
             )
 
         def mm_u(u, ts):
-            if ts[0] == 0:
+            if ("u", u) not in bacc:
                 x = acc_pool.tile([P, 4, P], F32, name="acc", tag="acc")
                 bacc["u", u] = x
             for t in ts:
@@ -200,7 +201,7 @@ def tile_dpo_like_hidden_step_s11_kernel(tc, h, r, beta, p_chosen, p_rejected, u
                     )
 
         def ev_u(u, eng):
-            if u % 4 == 0:
+            if (1, u // 4) not in gb:
                 x = grp_tile()
                 gb[1, u // 4] = x
             c = u % 4
@@ -234,17 +235,16 @@ def tile_dpo_like_hidden_step_s11_kernel(tc, h, r, beta, p_chosen, p_rejected, u
 
         gh, hbank = {}, {}
 
-        def tr_h(k):
-            for b in range(2):
-                x = tp_pool.tile([P, 2, 2, P], F32, name="tp", tag="tp")
-                for a in range(2):
-                    words = hraw[:, 2 * b + a, :].bitcast(F32)
-                    for u in range(2):
-                        nc.tensor.transpose(x[:, a, u, :], words[:, 256 * k + u : 256 * (k + 1) : 2], ident[:])
-                hbank[k, b] = x
+        def tr_h(k, b):
+            x = tp_pool.tile([P, 2, 2, P], F32, name="tp", tag="tp")
+            for a in range(2):
+                words = hraw[:, 2 * b + a, :].bitcast(F32)
+                for u in range(2):
+                    nc.tensor.transpose(x[:, a, u, :], words[:, 256 * k + u : 256 * (k + 1) : 2], ident[:])
+            hbank[k, b] = x
 
         def cp_h(k, b, eng):
-            if b == 0:
+            if k not in gh:
                 x = grp_tile()
                 gh[k] = x
             dst = gh[k][:, 256 * b : 256 * b + 256, :].rearrange("p c j -> p (c j)").bitcast(F32)
@@ -254,6 +254,8 @@ def tile_dpo_like_hidden_step_s11_kernel(tc, h, r, beta, p_chosen, p_rejected, u
             nc.vector.quantize_mx(
                 out=hcodes[k][:].bitcast(FP8X4), scales=hscales[k][:], in_=gh[k][:].rearrange("p c j -> p (c j)")
             )
+
+        macc = {}
 
         def mm_m(g, t):
             x = acc_pool.tile([P, 512], F32, name="acc", tag="acc")
@@ -268,7 +270,10 @@ def tile_dpo_like_hidden_step_s11_kernel(tc, h, r, beta, p_chosen, p_rejected, u
                     start=(k == 0),
                     stop=(k == ND - 1),
                 )
-            nc.scalar.activation(out=sig[g][:, t, :], in_=x[:], func=ACT.Sigmoid)
+            macc[g, t] = x
+
+        def sig_m(g, t):
+            nc.scalar.activation(out=sig[g][:, t, :], in_=macc[g, t][:], func=ACT.Sigmoid)
 
         ga = {}
 
@@ -315,135 +320,253 @@ def tile_dpo_like_hidden_step_s11_kernel(tc, h, r, beta, p_chosen, p_rejected, u
             move(eng, x[:, 0:w], oacc[i, c0][:, 0:w])
             nc.sync.dma_start(out=out[i * P : (i + 1) * P, c0 : c0 + w], in_=x[:, 0:w])
 
-        nc.vector.memset(usc[:].bitcast(I32), 0)
-        nc.gpsimd.memset(warm[:], 0.0)
-        nc.scalar.activation(out=warm[:], in_=warm[:], func=ACT.Sigmoid)
-        make_identity(nc, ident[:])
-        load_p(0, 2)
-        for rr in range(4):
-            nc.scalar.dma_start(
-                out=usc[rr:P:32, :, :].bitcast(I32),
-                in_=ut_scales[:, rr:16:4, :].rearrange("g q n -> q g n").bitcast(I32),
-            )
-        load_ut(ut0, 0)
-        load_p(1, 2)
-        load_ut(ut12, 1024)
+        def load_h():
+            nc.sync.dma_start(out=hraw[:], in_=h.rearrange("(i p) k -> p i k", p=P))
+
+        def load_beta():
+            nc.gpsimd.dma_start(out=beta_bf[:], in_=beta.rearrange("(g p t) -> p g t", g=NJ, t=4))
+
+        def cast_beta():
+            nc.vector.tensor_copy(out=beta_f[:], in_=beta_bf[:])
+
+        def load_usc(lo, hi, eng):
+            for rr in range(4):
+                (nc.scalar if eng == "s" else nc.sync).dma_start(
+                    out=usc[rr:P:32, :, lo:hi].bitcast(I32),
+                    in_=ut_scales[:, rr:16:4, lo:hi].rearrange("g q n -> q g n").bitcast(I32),
+                )
+
+        def load_u(n):
+            load_ut(ut0 if n == 0 else ut12, 0 if n == 0 else 1024)
+
+        def start():
+            nc.vector.memset(usc[:].bitcast(I32), 0)
+            nc.gpsimd.memset(warm[:], 0.0)
+            nc.scalar.activation(out=warm[:], in_=warm[:], func=ACT.Sigmoid)
+            make_identity(nc, ident[:])
+
+        start()
+        load_p(0)
+        sub(0, 1)
+        sub(0, 0)
+        load_usc(0, 1536, "y")
+        tr(0, 1)
+        load_p(1)
+        sub(1)
+        cp(0, 1, "s")
+        tr(0, 0)
+        quant_c(0, 1)
+        cp(0, 0, "s")
+        tr(1, 1)
+        quant_c(0, 0)
+        load_u(1)
+        tr(1, 0)
         load_p(2)
+        cp(1, 0, "s")
+        mm_b(0, 2)
+        load_u(0)
         load_r(0)
-        load_p(3)
-        nc.sync.dma_start(out=hraw[:], in_=h.rearrange("(i p) k -> p i k", p=P))
-        load_r(1)
-        load_r(2)
-        nc.gpsimd.dma_start(out=beta_bf[:], in_=beta.rearrange("(g p t) -> p g t", g=NJ, t=4))
-
-        def run_c(q, half=False):
-            for b in range(2):
-                tr(q, b)
-                cp(q, b, "s")
-                if half:
-                    quant_c(q, b)
-            if not half:
-                quant_c(q)
-
-        def mmev(q, n, eng="s"):
-            mm_b(q, n)
-            ev_b(q, n, eng)
-
-        def run_h(k):
-            tr_h(k)
-            cp_h(k, 0, "s")
-            cp_h(k, 1, "s")
-
-        def r_v(k, g):
-            inter_r(k, g, "v")
-
-        sub(0, 2)
-        load_p(4)
-        run_c(0, True)
-        sub(1, 2)
-        load_p(5)
-        mmev(0, 0)
-        run_c(1, True)
-        mmev(1, 0)
-        mmev(0, 1)
-        mmev(0, 2)
+        mm_b(0, 0)
+        ev_b(0, 2, "v")
+        cp(1, 1, "s")
         sub(2)
-        load_p(6)
-        mmev(1, 1)
-        run_c(2, True)
-        mmev(1, 2)
-        inter_r(0, 0, "v")
-        sub(3)
-        quant_r(0, 0)
-        load_p(7)
-        mmev(2, 0)
-        mmev(2, 1)
-        run_c(3, True)
-        nc.vector.tensor_copy(out=beta_f[:], in_=beta_bf[:])
+        quant_c(1)
+        tr(2, 0)
+        tr(2, 1)
+        cp(2, 1, "s")
+        mm_b(1, 1)
+        inter_r(0, 0, "s")
+        mm_b(1, 2)
         inter_r(0, 1, "v")
-        mmev(2, 2)
-        run_h(0)
-        quant_r(0, 1)
-        mmev(3, 0)
-        quant_h(0)
-        inter_r(1, 0, "v")
-        run_h(1)
-        quant_r(1, 0)
-        mmev(3, 1)
-        quant_h(1)
-        inter_r(2, 0, "v")
-        run_h(2)
-        mmev(3, 2)
-        quant_h(2)
-        quant_r(2, 0)
-        sub(4)
+        load_p(3)
+        load_r(1)
+        cp(2, 0, "v")
+        quant_c(2)
+        sub(3)
+        mm_b(1, 0)
+        ev_b(0, 0, "s")
+        quant_r(0, 0)
+        mm_b(2, 1)
+        ev_b(1, 1, "s")
+        tr(3, 0)
+        ev_b(1, 2, "s")
+        tr(3, 1)
+        mm_b(2, 0)
+        mm_b(2, 2)
         inter_r(1, 1, "s")
-        inter_r(2, 1, "v")
-        sub(5)
+        mm_b(0, 1)
+        load_h()
+        load_r(2)
+        ev_b(2, 1, "s")
+        inter_r(1, 0, "v")
+        quant_r(0, 1)
+        load_p(5)
+        cp(3, 0, "s")
+        ev_b(1, 0, "v")
+        tr_h(0, 0)
+        cp(3, 1, "s")
+        tr_h(0, 1)
+        ev_b(2, 0, "v")
+        tr_h(1, 1)
+        quant_r(1, 0)
+        cp_h(0, 0, "s")
         quant_r(1, 1)
+        quant_c(3)
+        cp_h(1, 1, "v")
+        mm_b(3, 0)
+        ev_b(0, 1, "s")
+        cp_h(0, 1, "s")
+        inter_r(2, 0, "v")
+        quant_h(0)
+        ev_b(2, 2, "s")
+        tr_h(1, 0)
+        tr_h(2, 1)
+        tr_h(2, 0)
+        quant_r(2, 0)
+        cp_h(1, 0, "s")
+        quant_h(1)
+        cp_h(2, 1, "s")
+        mm_b(3, 1)
+        cp_h(2, 0, "s")
+        quant_h(2)
+        load_beta()
+        mm_b(3, 2)
+        mm_m(0, 1)
+        mm_m(0, 0)
+        load_p(4)
+        ev_b(3, 0, "s")
+        cast_beta()
+        inter_r(2, 1, "s")
+        sub(5)
+        tr(5, 1)
+        sub(4)
+        ev_b(3, 1, "s")
+        load_p(6)
+        tr(5, 0)
+        cp(5, 1, "s")
+        tr(4, 0)
+        mm_m(0, 3)
+        mm_m(0, 2)
+        ev_b(3, 2, "s")
+        tr(4, 1)
         quant_r(2, 1)
-        for t in range(4):
-            mm_m(0, t)
-        for t in range(4):
-            run_c(4 + t)
-            mm_m(1, t)
-            if t < 2:
-                sub(6 + t)
-            if t == 2:
-                mul_a(0)
-        quant_a(0)
-        for u in range(3):
-            mm_u(u, [0, 1, 2])
+        cp(5, 0, "s")
+        sig_m(0, 0)
+        sub(6)
+        cp(4, 0, "v")
+        sig_m(0, 3)
+        quant_c(5)
+        tr(6, 0)
+        sig_m(0, 1)
+        tr(6, 1)
+        load_p(7)
+        cp(4, 1, "v")
+        sig_m(0, 2)
+        mm_m(1, 0)
+        mm_b(5, 0)
+        sig_m(1, 0)
+        mm_m(1, 1)
+        inter_b(0, 0, "s")
+        quant_c(4)
+        sub(7)
+        cp(6, 0, "v")
+        mm_m(1, 2)
+        cp(6, 1, "v")
+        quant_c(6)
+        sig_m(1, 1)
+        tr(7, 0)
+        sig_m(1, 2)
+        tr(7, 1)
+        ev_b(5, 0, "v")
+        cp(7, 0, "s")
+        cp(7, 1, "s")
+        quant_b(0, 0)
+        mm_b(4, 0)
+        mm_m(1, 3)
+        mul_a(0)
+        sig_m(1, 3)
+        mm_b(6, 0)
+        ev_b(4, 0, "s")
+        mm_b(6, 1)
+        ev_b(6, 0, "v")
+        quant_c(7)
         mul_a(1)
-        for u in range(3):
-            mm_u(u, [3])
-            ev_u(u, "s")
-            quant_u(u)
+        inter_b(0, 1, "s")
+        mm_b(5, 1)
+        ev_b(5, 1, "s")
+        mm_b(7, 0)
+        ev_b(7, 0, "s")
+        ev_b(6, 1, "s")
+        quant_a(0)
+        inter_b(0, 2, "s")
+        mm_b(7, 1)
+        mm_u(8, [0, 1, 2, 3])
+        mm_b(4, 1)
+        inter_b(1, 0, "v")
+        ev_b(7, 1, "s")
         quant_a(1)
-        for n in range(ND):
-            inter_b(0, n, "v")
-            u = 3 + n
-            mm_u(u, [0, 1, 2, 3])
-            ev_u(u, "s")
-            quant_u(u)
-            quant_b(0, n)
-
-        def out_chunk(c0, w, between=None):
-            for i in range(NT):
-                mm_o(i, c0, w, 0, "tp" if i < 2 else None)
-            for i in range(NT):
-                mm_o(i, c0, w, 1)
-                ev_o(i, c0, w, "s" if i % 2 == 0 else "v")
-
-        out_chunk(0, 512)
-        for u in range(6, 10):
-            mm_u(u, [0, 1, 2, 3])
-            ev_u(u, "s")
-            quant_u(u)
-        out_chunk(512, 512)
-        for u in range(10, 12):
-            mm_u(u, [0, 1, 2, 3])
-            ev_u(u, "s")
-            quant_u(u)
-        out_chunk(1024, 256)
-        out_chunk(1280, 256)
+        mm_u(9, [0, 1, 2, 3])
+        quant_b(1, 0)
+        quant_b(0, 2)
+        mm_o(3, 0, 512, 0)
+        mm_o(1, 0, 512, 0, "tp")
+        ev_b(4, 1, "s")
+        mm_o(0, 0, 512, 0, "tp")
+        mm_o(2, 0, 512, 0)
+        quant_b(0, 1)
+        mm_o(1, 0, 512, 1)
+        mm_o(2, 0, 512, 1)
+        mm_o(0, 0, 512, 1)
+        inter_b(1, 1, "v")
+        ev_u(9, "s")
+        ev_u(8, "s")
+        mm_o(3, 0, 512, 1)
+        quant_b(1, 1)
+        mm_o(3, 512, 512, 0)
+        ev_o(1, 0, 512, "s")
+        mm_o(0, 1024, 256, 0, "tp")
+        mm_u(11, [0, 1, 2, 3])
+        ev_o(2, 0, 512, "s")
+        ev_o(3, 0, 512, "s")
+        mm_o(1, 512, 512, 0, "tp")
+        mm_o(3, 1024, 256, 0)
+        quant_u(8)
+        quant_u(9)
+        mm_o(2, 1024, 256, 0)
+        ev_o(0, 0, 512, "v")
+        mm_o(3, 512, 512, 1)
+        mm_o(0, 1024, 256, 1)
+        mm_o(0, 512, 512, 0, "tp")
+        mm_o(1, 512, 512, 1)
+        ev_o(0, 1024, 256, "v")
+        mm_o(3, 1024, 256, 1)
+        mm_o(0, 512, 512, 1)
+        ev_o(3, 512, 512, "s")
+        ev_o(3, 1024, 256, "v")
+        ev_o(1, 512, 512, "v")
+        mm_u(10, [0, 1, 2, 3])
+        mm_o(2, 1024, 256, 1)
+        mm_o(1, 1024, 256, 0, "tp")
+        ev_u(11, "s")
+        ev_u(10, "s")
+        ev_o(0, 512, 512, "v")
+        quant_u(11)
+        mm_o(1, 1024, 256, 1)
+        ev_o(1, 1024, 256, "v")
+        mm_o(2, 512, 512, 0)
+        quant_u(10)
+        mm_o(2, 512, 512, 1)
+        mm_o(0, 1280, 256, 0, "tp")
+        ev_o(2, 1024, 256, "s")
+        ev_o(2, 512, 512, "s")
+        mm_o(3, 1280, 256, 0)
+        mm_o(2, 1280, 256, 0)
+        mm_o(2, 1280, 256, 1)
+        mm_o(0, 1280, 256, 1)
+        mm_o(3, 1280, 256, 1)
+        ev_o(0, 1280, 256, "s")
+        mm_o(1, 1280, 256, 0, "tp")
+        mm_o(1, 1280, 256, 1)
+        ev_o(3, 1280, 256, "s")
+        ev_o(1, 1280, 256, "v")
+        ev_o(2, 1280, 256, "v")

@@ -21,7 +21,7 @@ NV = V // 512
 ND = D // 512
 NJ = J // 512
 NT = T // P
-TPB = 3
+TPB = 2
 
 
 def tile_dpo_like_hidden_step_s11_kernel(tc, h, r, beta, p_chosen, p_rejected, ut_words, ut_scales, out):
@@ -38,9 +38,10 @@ def tile_dpo_like_hidden_step_s11_kernel(tc, h, r, beta, p_chosen, p_rejected, u
         beta_bf = keep.tile([P, NJ, 4], BF16, name="beta_bf")
         beta_f = keep.tile([P, NJ, 4], F32, name="beta_f")
         usc = keep.tile([P, NV, D], U8, name="usc", align_bytes=64)
-        ut0 = keep.tile([P, NV, 1024], U8, name="ut0", align_bytes=64)
-        ut12 = keep.tile([P, NV, 2048], U8, name="ut12", align_bytes=64)
+        uta = keep.tile([P, 2, 2 * D], U8, name="uta", align_bytes=64)
+        utb = keep.tile([P, 2, 2 * D], U8, name="utb", align_bytes=64)
         hraw = keep.tile([P, NT, D], BF16, name="hraw", align_bytes=64)
+        hre = keep.tile([P, NT, 2, D // 4, 2], BF16, name="hre", align_bytes=64)
         hcodes, hscales, rcodes, rscales = [], [], [], []
         for k in range(ND):
             t1 = keep.tile([P, T], U32, name="hc%d" % k, align_bytes=64)
@@ -71,8 +72,8 @@ def tile_dpo_like_hidden_step_s11_kernel(tc, h, r, beta, p_chosen, p_rejected, u
         def load_p(q, half=None):
             g, t = q // 4, q % 4
             if q not in pc:
-                a = work.tile([P, V], BF16, name="pc", tag="pc", bufs=4, align_bytes=64)
-                b = work.tile([P, V], BF16, name="pr", tag="pr", bufs=4, align_bytes=64)
+                a = work.tile([P, V], BF16, name="pc", tag="pc", bufs=3, align_bytes=64)
+                b = work.tile([P, V], BF16, name="pr", tag="pr", bufs=3, align_bytes=64)
                 pc[q], pr[q] = a, b
             cols = slice(0, V) if half is None else slice(half * V // 2, (half + 1) * V // 2)
             rows = slice(g * 512, (g + 1) * 512)
@@ -81,15 +82,9 @@ def tile_dpo_like_hidden_step_s11_kernel(tc, h, r, beta, p_chosen, p_rejected, u
             nc.sync.dma_start(out=pc[q][:, cols], in_=src_a[:, t, cols])
             nc.sync.dma_start(out=pr[q][:, cols], in_=src_b[:, t, cols])
 
-        def load_ut(dst, lo):
-            nc.sync.dma_start(
-                out=dst[:].bitcast(I32),
-                in_=ut_words[:, :, lo : lo + dst.shape[2]].rearrange("g p c -> p g c").bitcast(I32),
-            )
-
         def ut_cols(v, lo, w):
-            tile, at = (ut0, lo) if lo < 512 else (ut12, lo - 512)
-            return tile[:, v, 2 * at : 2 * (at + w)].bitcast(FP4X4)
+            tile = uta if v < 2 else utb
+            return tile[:, v % 2, 2 * lo : 2 * (lo + w)].bitcast(FP4X4)
 
         def load_r(k):
             x = work.tile([P, 4, J], BF16, name="rraw", tag="rraw", bufs=2, align_bytes=64)
@@ -147,11 +142,13 @@ def tile_dpo_like_hidden_step_s11_kernel(tc, h, r, beta, p_chosen, p_rejected, u
 
         bacc = {}
 
-        def mm_b(q, n):
-            x = acc_pool.tile([P, 512], F32, name="acc", tag="acc")
-            for v in range(NV):
+        def mm_b(q, n, half=None):
+            if (q, n) not in bacc:
+                x = acc_pool.tile([P, 512], F32, name="acc", tag="acc")
+                bacc[q, n] = x
+            for v in range(NV) if half is None else (2 * half, 2 * half + 1):
                 nc.tensor.matmul_mx(
-                    out=x[:],
+                    out=bacc[q, n][:],
                     lhsT=cc[q][:, v * P : (v + 1) * P].bitcast(FP8X4),
                     lhsT_scale=cs[q][:, v * P : (v + 1) * P],
                     rhs=ut_cols(v, n * 512, 512),
@@ -159,7 +156,6 @@ def tile_dpo_like_hidden_step_s11_kernel(tc, h, r, beta, p_chosen, p_rejected, u
                     start=(v == 0),
                     stop=(v == NV - 1),
                 )
-            bacc[q, n] = x
 
         def ev_b(q, n, eng):
             dst = braw if q < 4 else braw1
@@ -235,12 +231,20 @@ def tile_dpo_like_hidden_step_s11_kernel(tc, h, r, beta, p_chosen, p_rejected, u
 
         gh, hbank = {}, {}
 
+        def re_h(i, eng):
+            move(
+                eng,
+                hre[:, i, :, :, :],
+                hraw[:, i, :].rearrange("p (w u e) -> p u w e", u=2, e=2),
+            )
+
         def tr_h(k, b):
             x = tp_pool.tile([P, 2, 2, P], F32, name="tp", tag="tp")
             for a in range(2):
-                words = hraw[:, 2 * b + a, :].bitcast(F32)
+                words = hre[:, 2 * b + a, :, :, :].rearrange("p u w e -> p (u w e)").bitcast(F32)
                 for u in range(2):
-                    nc.tensor.transpose(x[:, a, u, :], words[:, 256 * k + u : 256 * (k + 1) : 2], ident[:])
+                    lo = u * (D // 4) + P * k
+                    nc.tensor.transpose(x[:, a, u, :], words[:, lo : lo + P], ident[:])
             hbank[k, b] = x
 
         def cp_h(k, b, eng):
@@ -314,7 +318,7 @@ def tile_dpo_like_hidden_step_s11_kernel(tc, h, r, beta, p_chosen, p_rejected, u
 
         def ev_o(i, c0, w, eng):
             if w == 512:
-                x = work.tile([P, 512], F32, name="osb", tag="osb", bufs=6, align_bytes=64)
+                x = work.tile([P, 512], F32, name="osb", tag="osb", bufs=5, align_bytes=64)
             else:
                 x = work.tile([P, 256], F32, name="osh", tag="osh", bufs=8, align_bytes=64)
             move(eng, x[:, 0:w], oacc[i, c0][:, 0:w])
@@ -324,7 +328,7 @@ def tile_dpo_like_hidden_step_s11_kernel(tc, h, r, beta, p_chosen, p_rejected, u
             nc.sync.dma_start(out=hraw[:], in_=h.rearrange("(i p) k -> p i k", p=P))
 
         def load_beta():
-            nc.gpsimd.dma_start(out=beta_bf[:], in_=beta.rearrange("(g p t) -> p g t", g=NJ, t=4))
+            nc.sync.dma_start(out=beta_bf[:], in_=beta.rearrange("(g p t) -> p g t", g=NJ, t=4))
 
         def cast_beta():
             nc.vector.tensor_copy(out=beta_f[:], in_=beta_bf[:])
@@ -336,237 +340,258 @@ def tile_dpo_like_hidden_step_s11_kernel(tc, h, r, beta, p_chosen, p_rejected, u
                     in_=ut_scales[:, rr:16:4, lo:hi].rearrange("g q n -> q g n").bitcast(I32),
                 )
 
-        def load_u(n):
-            load_ut(ut0 if n == 0 else ut12, 0 if n == 0 else 1024)
+        def load_u(half):
+            dst = uta if half == 0 else utb
+            nc.sync.dma_start(
+                out=dst[:].bitcast(I32),
+                in_=ut_words[2 * half : 2 * half + 2, :, :].rearrange("g p c -> p g c").bitcast(I32),
+            )
+
+        def zero_usc():
+            nc.vector.memset(usc[:].bitcast(I32), 0)
 
         def start():
-            nc.vector.memset(usc[:].bitcast(I32), 0)
             nc.gpsimd.memset(warm[:], 0.0)
             nc.scalar.activation(out=warm[:], in_=warm[:], func=ACT.Sigmoid)
             make_identity(nc, ident[:])
 
         start()
-        load_p(0)
+        load_p(0, 1)
+        load_p(0, 0)
+        zero_usc()
         sub(0, 1)
-        sub(0, 0)
-        load_usc(0, 1536, "y")
+        load_p(1, 0)
+        load_p(1, 1)
+        sub(1, 0)
         tr(0, 1)
-        load_p(1)
-        sub(1)
-        cp(0, 1, "s")
-        tr(0, 0)
-        quant_c(0, 1)
-        cp(0, 0, "s")
-        tr(1, 1)
-        quant_c(0, 0)
-        load_u(1)
-        tr(1, 0)
-        load_p(2)
-        cp(1, 0, "s")
-        mm_b(0, 2)
+        cp(0, 1, "v")
         load_u(0)
-        load_r(0)
-        mm_b(0, 0)
-        ev_b(0, 2, "v")
-        cp(1, 1, "s")
-        sub(2)
-        quant_c(1)
-        tr(2, 0)
-        tr(2, 1)
-        cp(2, 1, "s")
-        mm_b(1, 1)
-        inter_r(0, 0, "s")
-        mm_b(1, 2)
-        inter_r(0, 1, "v")
+        tr(1, 0)
+        sub(1, 1)
+        cp(1, 0, "s")
+        load_usc(0, 1536, "y")
+        sub(0, 0)
+        quant_c(1, 0)
+        load_u(1)
+        tr(1, 1)
+        load_p(2)
         load_p(3)
-        load_r(1)
+        tr(0, 0)
+        load_r(0)
+        cp(1, 1, "v")
+        quant_c(0, 1)
+        cp(0, 0, "v")
+        mm_b(1, 2, 0)
+        mm_b(1, 1, 0)
+        mm_b(1, 0, 0)
+        quant_c(0, 0)
+        quant_c(1, 1)
+        mm_b(1, 1, 1)
+        mm_b(0, 1, 0)
+        mm_b(1, 0, 1)
+        ev_b(1, 1, "v")
+        sub(2)
+        load_p(4)
+        mm_b(0, 0, 0)
+        mm_b(0, 1, 1)
+        tr(2, 1)
+        load_h()
+        ev_b(1, 0, "s")
+        tr(2, 0)
+        cp(2, 1, "s")
+        sub(3)
         cp(2, 0, "v")
         quant_c(2)
-        sub(3)
-        mm_b(1, 0)
-        ev_b(0, 0, "s")
+        mm_b(1, 2, 1)
+        mm_b(0, 0, 1)
+        tr(3, 1)
+        ev_b(1, 2, "s")
+        tr(3, 0)
+        load_r(1)
+        cp(3, 1, "s")
+        mm_b(0, 2, 0)
+        inter_r(0, 1, "v")
+        inter_r(0, 0, "s")
+        mm_b(2, 2)
+        cp(3, 0, "v")
+        mm_b(0, 2, 1)
+        sub(4)
+        quant_c(3)
+        quant_r(0, 1)
         quant_r(0, 0)
         mm_b(2, 1)
-        ev_b(1, 1, "s")
-        tr(3, 0)
-        ev_b(1, 2, "s")
-        tr(3, 1)
-        mm_b(2, 0)
-        mm_b(2, 2)
-        inter_r(1, 1, "s")
-        mm_b(0, 1)
-        load_h()
-        load_r(2)
-        ev_b(2, 1, "s")
-        inter_r(1, 0, "v")
-        quant_r(0, 1)
-        load_p(5)
-        cp(3, 0, "s")
-        ev_b(1, 0, "v")
-        tr_h(0, 0)
-        cp(3, 1, "s")
-        tr_h(0, 1)
-        ev_b(2, 0, "v")
-        tr_h(1, 1)
-        quant_r(1, 0)
-        cp_h(0, 0, "s")
-        quant_r(1, 1)
-        quant_c(3)
-        cp_h(1, 1, "v")
-        mm_b(3, 0)
-        ev_b(0, 1, "s")
-        cp_h(0, 1, "s")
-        inter_r(2, 0, "v")
-        quant_h(0)
-        ev_b(2, 2, "s")
-        tr_h(1, 0)
-        tr_h(2, 1)
-        tr_h(2, 0)
-        quant_r(2, 0)
-        cp_h(1, 0, "s")
-        quant_h(1)
-        cp_h(2, 1, "s")
-        mm_b(3, 1)
-        cp_h(2, 0, "s")
-        quant_h(2)
-        load_beta()
-        mm_b(3, 2)
-        mm_m(0, 1)
-        mm_m(0, 0)
-        load_p(4)
-        ev_b(3, 0, "s")
-        cast_beta()
-        inter_r(2, 1, "s")
-        sub(5)
-        tr(5, 1)
-        sub(4)
-        ev_b(3, 1, "s")
-        load_p(6)
-        tr(5, 0)
-        cp(5, 1, "s")
-        tr(4, 0)
-        mm_m(0, 3)
-        mm_m(0, 2)
-        ev_b(3, 2, "s")
         tr(4, 1)
-        quant_r(2, 1)
-        cp(5, 0, "s")
-        sig_m(0, 0)
-        sub(6)
-        cp(4, 0, "v")
-        sig_m(0, 3)
-        quant_c(5)
-        tr(6, 0)
-        sig_m(0, 1)
-        tr(6, 1)
-        load_p(7)
+        tr(4, 0)
+        ev_b(0, 1, "s")
         cp(4, 1, "v")
-        sig_m(0, 2)
-        mm_m(1, 0)
-        mm_b(5, 0)
-        sig_m(1, 0)
-        mm_m(1, 1)
-        inter_b(0, 0, "s")
+        mm_b(3, 1)
+        load_r(2)
+        re_h(2, "v")
+        ev_b(0, 0, "s")
+        ev_b(2, 2, "s")
+        cp(4, 0, "v")
+        ev_b(0, 2, "s")
+        mm_b(3, 2)
+        re_h(3, "s")
+        ev_b(2, 1, "s")
+        tr_h(2, 1)
+        re_h(1, "v")
+        tr_h(1, 1)
+        mm_b(3, 0)
+        re_h(0, "v")
+        ev_b(3, 2, "s")
+        cp_h(2, 1, "s")
         quant_c(4)
-        sub(7)
-        cp(6, 0, "v")
-        mm_m(1, 2)
-        cp(6, 1, "v")
-        quant_c(6)
-        sig_m(1, 1)
-        tr(7, 0)
-        sig_m(1, 2)
-        tr(7, 1)
-        ev_b(5, 0, "v")
-        cp(7, 0, "s")
-        cp(7, 1, "s")
-        quant_b(0, 0)
-        mm_b(4, 0)
-        mm_m(1, 3)
-        mul_a(0)
-        sig_m(1, 3)
-        mm_b(6, 0)
-        ev_b(4, 0, "s")
-        mm_b(6, 1)
-        ev_b(6, 0, "v")
-        quant_c(7)
-        mul_a(1)
-        inter_b(0, 1, "s")
-        mm_b(5, 1)
-        ev_b(5, 1, "s")
-        mm_b(7, 0)
-        ev_b(7, 0, "s")
-        ev_b(6, 1, "s")
-        quant_a(0)
-        inter_b(0, 2, "s")
-        mm_b(7, 1)
-        mm_u(8, [0, 1, 2, 3])
+        cp_h(1, 1, "s")
+        tr_h(2, 0)
+        ev_b(3, 1, "s")
+        cp_h(2, 0, "s")
+        tr_h(1, 0)
+        load_p(5)
         mm_b(4, 1)
-        inter_b(1, 0, "v")
-        ev_b(7, 1, "s")
-        quant_a(1)
-        mm_u(9, [0, 1, 2, 3])
-        quant_b(1, 0)
-        quant_b(0, 2)
-        mm_o(3, 0, 512, 0)
-        mm_o(1, 0, 512, 0, "tp")
+        tr_h(0, 0)
+        inter_r(1, 1, "v")
+        mm_b(2, 0)
+        cp_h(1, 0, "v")
+        tr_h(0, 1)
+        mm_b(4, 0)
+        quant_r(1, 1)
+        inter_r(2, 1, "s")
+        quant_h(2)
+        quant_h(1)
+        load_p(6)
+        load_beta()
+        cp_h(0, 0, "s")
+        sub(5)
+        cp_h(0, 1, "s")
+        quant_r(2, 1)
+        tr(5, 0)
+        ev_b(3, 0, "s")
         ev_b(4, 1, "s")
+        cp(5, 0, "s")
+        tr(5, 1)
+        ev_b(2, 0, "s")
+        quant_h(0)
+        sub(6)
+        mm_m(1, 3)
+        mm_m(1, 2)
+        mm_m(1, 1)
+        cp(5, 1, "s")
+        inter_r(1, 0, "s")
+        inter_r(2, 0, "v")
+        tr(6, 0)
+        tr(6, 1)
+        mm_m(1, 0)
+        ev_b(4, 0, "v")
+        quant_c(5)
+        quant_r(2, 0)
+        quant_r(1, 0)
+        sig_m(1, 1)
+        cp(6, 0, "s")
+        cp(6, 1, "s")
+        sig_m(1, 3)
+        load_p(7)
+        mm_b(5, 1)
+        mm_b(5, 0)
+        sub(7)
+        tr(7, 1)
+        sig_m(1, 2)
+        quant_c(6)
+        sig_m(1, 0)
+        cp(7, 1, "s")
+        ev_b(5, 0, "s")
+        cast_beta()
+        tr(7, 0)
+        mm_m(0, 1)
+        inter_b(0, 0, "v")
+        mm_m(0, 0)
+        ev_b(5, 1, "s")
+        cp(7, 0, "s")
+        mm_m(0, 2)
+        mm_m(0, 3)
+        sig_m(0, 1)
+        mul_a(1)
+        mm_b(6, 0)
+        sig_m(0, 2)
+        quant_c(7)
+        quant_b(0, 0)
+        mm_b(7, 0)
+        quant_a(1)
+        sig_m(0, 0)
+        sig_m(0, 3)
+        ev_b(6, 0, "s")
+        ev_b(7, 0, "s")
+        mul_a(0)
+        inter_b(1, 0, "v")
+        quant_a(0)
+        quant_b(1, 0)
+        mm_u(11, [0, 1, 2, 3])
+        mm_b(7, 1)
+        mm_u(10, [0, 1, 2, 3])
+        mm_b(6, 1)
+        inter_b(0, 2, "v")
+        inter_b(0, 1, "s")
         mm_o(0, 0, 512, 0, "tp")
         mm_o(2, 0, 512, 0)
-        quant_b(0, 1)
-        mm_o(1, 0, 512, 1)
-        mm_o(2, 0, 512, 1)
-        mm_o(0, 0, 512, 1)
-        inter_b(1, 1, "v")
-        ev_u(9, "s")
-        ev_u(8, "s")
-        mm_o(3, 0, 512, 1)
-        quant_b(1, 1)
-        mm_o(3, 512, 512, 0)
-        ev_o(1, 0, 512, "s")
-        mm_o(0, 1024, 256, 0, "tp")
-        mm_u(11, [0, 1, 2, 3])
-        ev_o(2, 0, 512, "s")
-        ev_o(3, 0, 512, "s")
-        mm_o(1, 512, 512, 0, "tp")
-        mm_o(3, 1024, 256, 0)
-        quant_u(8)
-        quant_u(9)
-        mm_o(2, 1024, 256, 0)
-        ev_o(0, 0, 512, "v")
-        mm_o(3, 512, 512, 1)
-        mm_o(0, 1024, 256, 1)
-        mm_o(0, 512, 512, 0, "tp")
-        mm_o(1, 512, 512, 1)
-        ev_o(0, 1024, 256, "v")
-        mm_o(3, 1024, 256, 1)
-        mm_o(0, 512, 512, 1)
-        ev_o(3, 512, 512, "s")
-        ev_o(3, 1024, 256, "v")
-        ev_o(1, 512, 512, "v")
-        mm_u(10, [0, 1, 2, 3])
-        mm_o(2, 1024, 256, 1)
-        mm_o(1, 1024, 256, 0, "tp")
         ev_u(11, "s")
+        ev_b(7, 1, "s")
         ev_u(10, "s")
-        ev_o(0, 512, 512, "v")
+        mm_o(0, 0, 512, 1)
+        mm_o(3, 0, 512, 0)
+        mm_o(1, 0, 512, 0, "tp")
+        mm_o(1, 0, 512, 1)
+        ev_b(6, 1, "s")
         quant_u(11)
-        mm_o(1, 1024, 256, 1)
-        ev_o(1, 1024, 256, "v")
-        mm_o(2, 512, 512, 0)
+        ev_o(0, 0, 512, "s")
+        quant_b(0, 2)
+        mm_o(3, 0, 512, 1)
+        mm_u(8, [0, 1, 2, 3])
+        ev_o(1, 0, 512, "s")
         quant_u(10)
-        mm_o(2, 512, 512, 1)
-        mm_o(0, 1280, 256, 0, "tp")
-        ev_o(2, 1024, 256, "s")
-        ev_o(2, 512, 512, "s")
         mm_o(3, 1280, 256, 0)
-        mm_o(2, 1280, 256, 0)
-        mm_o(2, 1280, 256, 1)
-        mm_o(0, 1280, 256, 1)
-        mm_o(3, 1280, 256, 1)
-        ev_o(0, 1280, 256, "s")
+        inter_b(1, 1, "v")
         mm_o(1, 1280, 256, 0, "tp")
         mm_o(1, 1280, 256, 1)
+        mm_o(0, 1280, 256, 0, "tp")
+        ev_o(3, 0, 512, "s")
+        mm_o(3, 1280, 256, 1)
+        mm_o(2, 0, 512, 1)
+        quant_b(0, 1)
+        quant_b(1, 1)
+        ev_u(8, "s")
+        ev_o(1, 1280, 256, "s")
+        mm_o(2, 1280, 256, 0)
         ev_o(3, 1280, 256, "s")
-        ev_o(1, 1280, 256, "v")
-        ev_o(2, 1280, 256, "v")
+        mm_o(2, 1280, 256, 1)
+        mm_o(0, 1280, 256, 1)
+        ev_o(0, 1280, 256, "v")
+        ev_o(2, 0, 512, "s")
+        mm_u(9, [0, 1, 2, 3])
+        quant_u(8)
+        mm_o(0, 512, 512, 0, "tp")
+        ev_o(2, 1280, 256, "s")
+        mm_o(0, 512, 512, 1)
+        ev_u(9, "v")
+        mm_o(2, 512, 512, 0)
+        ev_o(0, 512, 512, "s")
+        mm_o(2, 512, 512, 1)
+        quant_u(9)
+        mm_o(1, 512, 512, 0, "tp")
+        mm_o(1, 512, 512, 1)
+        ev_o(2, 512, 512, "v")
+        ev_o(1, 512, 512, "s")
+        mm_o(3, 512, 512, 0)
+        mm_o(3, 512, 512, 1)
+        ev_o(3, 512, 512, "v")
+        mm_o(0, 1024, 256, 0, "tp")
+        mm_o(2, 1024, 256, 0)
+        mm_o(3, 1024, 256, 0)
+        mm_o(3, 1024, 256, 1)
+        mm_o(0, 1024, 256, 1)
+        mm_o(2, 1024, 256, 1)
+        ev_o(3, 1024, 256, "v")
+        mm_o(1, 1024, 256, 0, "tp")
+        mm_o(1, 1024, 256, 1)
+        ev_o(1, 1024, 256, "v")
+        ev_o(2, 1024, 256, "s")
+        ev_o(0, 1024, 256, "s")

from contextlib import ExitStack

import concourse.mybir as mybir
from concourse.masks import make_identity

T, D, J, V = 512, 1536, 1024, 2048
P = 128
FLOPS = 2 * (T * D * J + J * V * D + T * J * D)

F32 = mybir.dt.float32
BF16 = mybir.dt.bfloat16
I32 = mybir.dt.int32
U32 = mybir.dt.uint32
U8 = mybir.dt.uint8
FP8X4 = mybir.dt.float8_e4m3fn_x4
FP4X4 = mybir.dt.float4_e2m1fn_x4
ACT = mybir.ActivationFunctionType
ALU = mybir.AluOpType

NV = V // 512
ND = D // 512
NJ = J // 512
NT = T // P
TPB = 2


def tile_dpo_like_hidden_step_s11_kernel(tc, h, r, beta, p_chosen, p_rejected, ut_words, ut_scales, out):
    nc = tc.nc
    with ExitStack() as ctx:
        keep = ctx.enter_context(tc.tile_pool(name="keep", bufs=1))
        work = ctx.enter_context(tc.tile_pool(name="work", bufs=2))
        tp_pool = ctx.enter_context(tc.psum_pool(name="tp_pool", bufs=TPB))
        acc_pool = ctx.enter_context(tc.psum_pool(name="acc_pool", bufs=8 - TPB))
        ctx.enter_context(tc.manual_schedule())

        ident = keep.tile([P, P], F32, name="ident")
        warm = keep.tile([P, 1], F32, name="warm")
        beta_bf = keep.tile([P, NJ, 4], BF16, name="beta_bf")
        beta_f = keep.tile([P, NJ, 4], F32, name="beta_f")
        usc = keep.tile([P, NV, D], U8, name="usc", align_bytes=64)
        uta = keep.tile([P, 2, 2 * D], U8, name="uta", align_bytes=64)
        utb = keep.tile([P, 2, 2 * D], U8, name="utb", align_bytes=64)
        hraw = keep.tile([P, NT, D], BF16, name="hraw", align_bytes=64)
        hre = keep.tile([P, NT, 2, D // 4, 2], BF16, name="hre", align_bytes=64)
        hcodes, hscales, rcodes, rscales = [], [], [], []
        for k in range(ND):
            t1 = keep.tile([P, T], U32, name="hc%d" % k, align_bytes=64)
            t2 = keep.tile([P, T], U8, name="hs%d" % k, align_bytes=64)
            t3 = keep.tile([P, J], U32, name="rc%d" % k, align_bytes=64)
            t4 = keep.tile([P, J], U8, name="rs%d" % k, align_bytes=64)
            hcodes.append(t1)
            hscales.append(t2)
            rcodes.append(t3)
            rscales.append(t4)
        acodes, ascales, bcodes, bscales, sig = [], [], [], [], []
        braw = keep.tile([P, 4, D], BF16, name="braw", align_bytes=64)
        braw1 = keep.tile([P, 4, 1024], BF16, name="braw1", align_bytes=64)
        for g in range(NJ):
            t1 = keep.tile([P, T], U32, name="ac%d" % g, align_bytes=64)
            t2 = keep.tile([P, T], U8, name="as%d" % g, align_bytes=64)
            t3 = keep.tile([P, D], U32, name="bc%d" % g, align_bytes=64)
            t4 = keep.tile([P, D], U8, name="bs%d" % g, align_bytes=64)
            t6 = keep.tile([P, 4, T], F32, name="sig%d" % g, align_bytes=64)
            acodes.append(t1)
            ascales.append(t2)
            bcodes.append(t3)
            bscales.append(t4)
            sig.append(t6)

        pc, pr, rraw = {}, {}, {}

        def load_p(q, half=None):
            g, t = q // 4, q % 4
            if q not in pc:
                a = work.tile([P, V], BF16, name="pc", tag="pc", bufs=3, align_bytes=64)
                b = work.tile([P, V], BF16, name="pr", tag="pr", bufs=3, align_bytes=64)
                pc[q], pr[q] = a, b
            cols = slice(0, V) if half is None else slice(half * V // 2, (half + 1) * V // 2)
            rows = slice(g * 512, (g + 1) * 512)
            src_a = p_chosen[rows, :].rearrange("(m t) v -> m t v", t=4)
            src_b = p_rejected[rows, :].rearrange("(m t) v -> m t v", t=4)
            nc.sync.dma_start(out=pc[q][:, cols], in_=src_a[:, t, cols])
            nc.sync.dma_start(out=pr[q][:, cols], in_=src_b[:, t, cols])

        def ut_cols(v, lo, w):
            tile = uta if v < 2 else utb
            return tile[:, v % 2, 2 * lo : 2 * (lo + w)].bitcast(FP4X4)

        def load_r(k):
            x = work.tile([P, 4, J], BF16, name="rraw", tag="rraw", bufs=2, align_bytes=64)
            nc.sync.dma_start(out=x[:], in_=r[k * 512 : (k + 1) * 512, :].rearrange("(p j) c -> p j c", j=4))
            rraw[k] = x

        diff, ct, cc, cs = {}, {}, {}, {}

        def sub(q, half=None):
            if q not in diff:
                x = work.tile([P, 2, V // 4, 2], BF16, name="diff", tag="diff", bufs=2, align_bytes=64)
                diff[q] = x
            lo, hi = (0, V) if half is None else (half * V // 2, (half + 1) * V // 2)
            nc.vector.tensor_tensor(
                out=diff[q][:, :, lo // 4 : hi // 4, :],
                in0=pc[q][:, lo:hi].rearrange("p (w u e) -> p u w e", u=2, e=2),
                in1=pr[q][:, lo:hi].rearrange("p (w u e) -> p u w e", u=2, e=2),
                op=ALU.subtract,
            )

        bank = {}

        def tr(q, b):
            words = diff[q][:].rearrange("p u w e -> p (u w e)").bitcast(F32)
            x = tp_pool.tile([P, 2, 2, P], F32, name="tp", tag="tp")
            for a in range(2):
                for u in range(2):
                    lo = u * 512 + (2 * b + a) * P
                    nc.tensor.transpose(x[:, a, u, :], words[:, lo : lo + P], ident[:])
            bank[q, b] = x

        def cp(q, b, eng):
            if q not in ct:
                x = work.tile([P, NV, P, 4], BF16, name="ct", tag="ct", bufs=2, align_bytes=64)
                ct[q] = x
            dst = ct[q][:, 2 * b : 2 * b + 2, :, :].rearrange("p a r j -> p (a r j)").bitcast(F32)
            move(eng, dst.rearrange("p (a r u) -> p a r u", a=2, u=2), bank[q, b][:].rearrange("p a u r -> p a r u"))

        def move(eng, dst, src):
            if eng == "s":
                nc.scalar.copy(out=dst, in_=src)
            else:
                nc.vector.tensor_copy(out=dst, in_=src)

        def quant_c(q, half=None):
            if q not in cc:
                x = work.tile([P, NV * P], U32, name="cc", tag="cc", bufs=6, align_bytes=64)
                y = work.tile([P, NV * P], U8, name="cs", tag="cs", bufs=6, align_bytes=64)
                cc[q], cs[q] = x, y
            flat = ct[q][:].rearrange("p a r j -> p (a r j)")
            lo, hi = (0, 512) if half is None else (256 * half, 256 * half + 256)
            nc.vector.quantize_mx(
                out=cc[q][:, lo:hi].bitcast(FP8X4), scales=cs[q][:, lo:hi], in_=flat[:, 4 * lo : 4 * hi]
            )

        bacc = {}

        def mm_b(q, n, half=None):
            if (q, n) not in bacc:
                x = acc_pool.tile([P, 512], F32, name="acc", tag="acc")
                bacc[q, n] = x
            for v in range(NV) if half is None else (2 * half, 2 * half + 1):
                nc.tensor.matmul_mx(
                    out=bacc[q, n][:],
                    lhsT=cc[q][:, v * P : (v + 1) * P].bitcast(FP8X4),
                    lhsT_scale=cs[q][:, v * P : (v + 1) * P],
                    rhs=ut_cols(v, n * 512, 512),
                    rhs_scale=usc[:, v, n * 512 : (n + 1) * 512],
                    start=(v == 0),
                    stop=(v == NV - 1),
                )

        def ev_b(q, n, eng):
            dst = braw if q < 4 else braw1
            move(eng, dst[:, q % 4, n * 512 : (n + 1) * 512], bacc[q, n][:])

        def grp_tile():
            x = work.tile([P, 512, 4], BF16, name="grp", tag="grp", bufs=6, align_bytes=64)
            return x

        gb = {}

        def inter_b(g, n, eng):
            x = grp_tile()
            src = braw if g == 0 else braw1
            move(eng, x[:], src[:, :, n * 512 : (n + 1) * 512].rearrange("p t n -> p n t"))
            gb[g, n] = x

        def quant_b(g, n):
            cols = slice(n * 512, (n + 1) * 512)
            nc.vector.quantize_mx(
                out=bcodes[g][:, cols].bitcast(FP8X4), scales=bscales[g][:, cols],
                in_=gb[g, n][:].rearrange("p c j -> p (c j)"),
            )

        def mm_u(u, ts):
            if ("u", u) not in bacc:
                x = acc_pool.tile([P, 4, P], F32, name="acc", tag="acc")
                bacc["u", u] = x
            for t in ts:
                for v in range(NV):
                    nc.tensor.matmul_mx(
                        out=bacc["u", u][:, t, :],
                        lhsT=cc[4 + t][:, v * P : (v + 1) * P].bitcast(FP8X4),
                        lhsT_scale=cs[4 + t][:, v * P : (v + 1) * P],
                        rhs=ut_cols(v, u * P, P),
                        rhs_scale=usc[:, v, u * P : (u + 1) * P],
                        start=(v == 0),
                        stop=(v == NV - 1),
                    )

        def ev_u(u, eng):
            if (1, u // 4) not in gb:
                x = grp_tile()
                gb[1, u // 4] = x
            c = u % 4
            move(eng, gb[1, u // 4][:, c * P : (c + 1) * P, :], bacc["u", u][:].rearrange("p t n -> p n t"))

        def quant_u(u):
            cols = slice(u * P, (u + 1) * P)
            c = u % 4
            nc.vector.quantize_mx(
                out=bcodes[1][:, cols].bitcast(FP8X4), scales=bscales[1][:, cols],
                in_=gb[1, u // 4][:, c * P : (c + 1) * P, :].rearrange("p c j -> p (c j)"),
            )

        gr = {}

        def inter_r(k, g, eng):
            x = grp_tile()
            move(
                eng,
                x[:].rearrange("p (t m) j -> p t m j", t=4),
                rraw[k][:, :, g * 512 : (g + 1) * 512].rearrange("p j (m t) -> p t m j", t=4),
            )
            gr[k, g] = x

        def quant_r(k, g):
            cols = slice(g * 512, (g + 1) * 512)
            nc.vector.quantize_mx(
                out=rcodes[k][:, cols].bitcast(FP8X4), scales=rscales[k][:, cols],
                in_=gr[k, g][:].rearrange("p c j -> p (c j)"),
            )

        gh, hbank = {}, {}

        def re_h(i, eng):
            move(
                eng,
                hre[:, i, :, :, :],
                hraw[:, i, :].rearrange("p (w u e) -> p u w e", u=2, e=2),
            )

        def tr_h(k, b):
            x = tp_pool.tile([P, 2, 2, P], F32, name="tp", tag="tp")
            for a in range(2):
                words = hre[:, 2 * b + a, :, :, :].rearrange("p u w e -> p (u w e)").bitcast(F32)
                for u in range(2):
                    lo = u * (D // 4) + P * k
                    nc.tensor.transpose(x[:, a, u, :], words[:, lo : lo + P], ident[:])
            hbank[k, b] = x

        def cp_h(k, b, eng):
            if k not in gh:
                x = grp_tile()
                gh[k] = x
            dst = gh[k][:, 256 * b : 256 * b + 256, :].rearrange("p c j -> p (c j)").bitcast(F32)
            move(eng, dst.rearrange("p (a r u) -> p a r u", a=2, u=2), hbank[k, b][:].rearrange("p a u r -> p a r u"))

        def quant_h(k):
            nc.vector.quantize_mx(
                out=hcodes[k][:].bitcast(FP8X4), scales=hscales[k][:], in_=gh[k][:].rearrange("p c j -> p (c j)")
            )

        macc = {}

        def mm_m(g, t):
            x = acc_pool.tile([P, 512], F32, name="acc", tag="acc")
            cols = slice(g * 512 + t * P, g * 512 + (t + 1) * P)
            for k in range(ND):
                nc.tensor.matmul_mx(
                    out=x[:],
                    lhsT=rcodes[k][:, cols].bitcast(FP8X4),
                    lhsT_scale=rscales[k][:, cols],
                    rhs=hcodes[k][:].bitcast(FP8X4),
                    rhs_scale=hscales[k][:],
                    start=(k == 0),
                    stop=(k == ND - 1),
                )
            macc[g, t] = x

        def sig_m(g, t):
            nc.scalar.activation(out=sig[g][:, t, :], in_=macc[g, t][:], func=ACT.Sigmoid)

        ga = {}

        def mul_a(g):
            x = grp_tile()
            nc.vector.tensor_tensor(
                out=x[:],
                in0=sig[g][:].rearrange("p t n -> p n t"),
                in1=beta_f[:, g : g + 1, :].to_broadcast([P, T, 4]),
                op=ALU.mult,
            )
            ga[g] = x

        def quant_a(g):
            nc.vector.quantize_mx(
                out=acodes[g][:].bitcast(FP8X4), scales=ascales[g][:], in_=ga[g][:].rearrange("p c j -> p (c j)")
            )

        oacc = {}

        def mm_o(i, c0, w, g, pool=None):
            if g == 0:
                if pool == "tp":
                    x = tp_pool.tile([P, 512], F32, name="tp", tag="tp")
                else:
                    x = acc_pool.tile([P, 512], F32, name="acc", tag="acc")
                oacc[i, c0] = x
            rows, cols = slice(i * P, (i + 1) * P), slice(c0, c0 + w)
            nc.tensor.matmul_mx(
                out=oacc[i, c0][:, 0:w],
                lhsT=acodes[g][:, rows].bitcast(FP8X4),
                lhsT_scale=ascales[g][:, rows],
                rhs=bcodes[g][:, cols].bitcast(FP8X4),
                rhs_scale=bscales[g][:, cols],
                start=(g == 0),
                stop=(g == NJ - 1),
            )

        def ev_o(i, c0, w, eng):
            if w == 512:
                x = work.tile([P, 512], F32, name="osb", tag="osb", bufs=5, align_bytes=64)
            else:
                x = work.tile([P, 256], F32, name="osh", tag="osh", bufs=8, align_bytes=64)
            move(eng, x[:, 0:w], oacc[i, c0][:, 0:w])
            nc.sync.dma_start(out=out[i * P : (i + 1) * P, c0 : c0 + w], in_=x[:, 0:w])

        def load_h():
            nc.sync.dma_start(out=hraw[:], in_=h.rearrange("(i p) k -> p i k", p=P))

        def load_beta():
            nc.sync.dma_start(out=beta_bf[:], in_=beta.rearrange("(g p t) -> p g t", g=NJ, t=4))

        def cast_beta():
            nc.vector.tensor_copy(out=beta_f[:], in_=beta_bf[:])

        def load_usc(lo, hi, eng):
            for rr in range(4):
                (nc.scalar if eng == "s" else nc.sync).dma_start(
                    out=usc[rr:P:32, :, lo:hi].bitcast(I32),
                    in_=ut_scales[:, rr:16:4, lo:hi].rearrange("g q n -> q g n").bitcast(I32),
                )

        def load_u(half):
            dst = uta if half == 0 else utb
            nc.sync.dma_start(
                out=dst[:].bitcast(I32),
                in_=ut_words[2 * half : 2 * half + 2, :, :].rearrange("g p c -> p g c").bitcast(I32),
            )

        def zero_usc():
            nc.vector.memset(usc[:].bitcast(I32), 0)

        def start():
            nc.gpsimd.memset(warm[:], 0.0)
            nc.scalar.activation(out=warm[:], in_=warm[:], func=ACT.Sigmoid)
            make_identity(nc, ident[:])

        start()
        load_p(0, 1)
        load_p(0, 0)
        zero_usc()
        sub(0, 1)
        load_p(1, 0)
        load_p(1, 1)
        sub(1, 0)
        tr(0, 1)
        cp(0, 1, "v")
        load_u(0)
        tr(1, 0)
        sub(1, 1)
        cp(1, 0, "s")
        load_usc(0, 1536, "y")
        sub(0, 0)
        quant_c(1, 0)
        load_u(1)
        tr(1, 1)
        load_p(2)
        load_p(3)
        tr(0, 0)
        load_r(0)
        cp(1, 1, "v")
        quant_c(0, 1)
        cp(0, 0, "v")
        mm_b(1, 2, 0)
        mm_b(1, 1, 0)
        mm_b(1, 0, 0)
        quant_c(0, 0)
        quant_c(1, 1)
        mm_b(1, 1, 1)
        mm_b(0, 1, 0)
        mm_b(1, 0, 1)
        ev_b(1, 1, "v")
        sub(2)
        load_p(4)
        mm_b(0, 0, 0)
        mm_b(0, 1, 1)
        tr(2, 1)
        load_h()
        ev_b(1, 0, "s")
        tr(2, 0)
        cp(2, 1, "s")
        sub(3)
        cp(2, 0, "v")
        quant_c(2)
        mm_b(1, 2, 1)
        mm_b(0, 0, 1)
        tr(3, 1)
        ev_b(1, 2, "s")
        tr(3, 0)
        load_r(1)
        cp(3, 1, "s")
        mm_b(0, 2, 0)
        inter_r(0, 1, "v")
        inter_r(0, 0, "s")
        mm_b(2, 2)
        cp(3, 0, "v")
        mm_b(0, 2, 1)
        sub(4)
        quant_c(3)
        quant_r(0, 1)
        quant_r(0, 0)
        mm_b(2, 1)
        tr(4, 1)
        tr(4, 0)
        ev_b(0, 1, "s")
        cp(4, 1, "v")
        mm_b(3, 1)
        load_r(2)
        re_h(2, "v")
        ev_b(0, 0, "s")
        ev_b(2, 2, "s")
        cp(4, 0, "v")
        ev_b(0, 2, "s")
        mm_b(3, 2)
        re_h(3, "s")
        ev_b(2, 1, "s")
        tr_h(2, 1)
        re_h(1, "v")
        tr_h(1, 1)
        mm_b(3, 0)
        re_h(0, "v")
        ev_b(3, 2, "s")
        cp_h(2, 1, "s")
        quant_c(4)
        cp_h(1, 1, "s")
        tr_h(2, 0)
        ev_b(3, 1, "s")
        cp_h(2, 0, "s")
        tr_h(1, 0)
        load_p(5)
        mm_b(4, 1)
        tr_h(0, 0)
        inter_r(1, 1, "v")
        mm_b(2, 0)
        cp_h(1, 0, "v")
        tr_h(0, 1)
        mm_b(4, 0)
        quant_r(1, 1)
        inter_r(2, 1, "s")
        quant_h(2)
        quant_h(1)
        load_p(6)
        load_beta()
        cp_h(0, 0, "s")
        sub(5)
        cp_h(0, 1, "s")
        quant_r(2, 1)
        tr(5, 0)
        ev_b(3, 0, "s")
        ev_b(4, 1, "s")
        cp(5, 0, "s")
        tr(5, 1)
        ev_b(2, 0, "s")
        quant_h(0)
        sub(6)
        mm_m(1, 3)
        mm_m(1, 2)
        mm_m(1, 1)
        cp(5, 1, "s")
        inter_r(1, 0, "s")
        inter_r(2, 0, "v")
        tr(6, 0)
        tr(6, 1)
        mm_m(1, 0)
        ev_b(4, 0, "v")
        quant_c(5)
        quant_r(2, 0)
        quant_r(1, 0)
        sig_m(1, 1)
        cp(6, 0, "s")
        cp(6, 1, "s")
        sig_m(1, 3)
        load_p(7)
        mm_b(5, 1)
        mm_b(5, 0)
        sub(7)
        tr(7, 1)
        sig_m(1, 2)
        quant_c(6)
        sig_m(1, 0)
        cp(7, 1, "s")
        ev_b(5, 0, "s")
        cast_beta()
        tr(7, 0)
        mm_m(0, 1)
        inter_b(0, 0, "v")
        mm_m(0, 0)
        ev_b(5, 1, "s")
        cp(7, 0, "s")
        mm_m(0, 2)
        mm_m(0, 3)
        sig_m(0, 1)
        mul_a(1)
        mm_b(6, 0)
        sig_m(0, 2)
        quant_c(7)
        quant_b(0, 0)
        mm_b(7, 0)
        quant_a(1)
        sig_m(0, 0)
        sig_m(0, 3)
        ev_b(6, 0, "s")
        ev_b(7, 0, "s")
        mul_a(0)
        inter_b(1, 0, "v")
        quant_a(0)
        quant_b(1, 0)
        mm_u(11, [0, 1, 2, 3])
        mm_b(7, 1)
        mm_u(10, [0, 1, 2, 3])
        mm_b(6, 1)
        inter_b(0, 2, "v")
        inter_b(0, 1, "s")
        mm_o(0, 0, 512, 0, "tp")
        mm_o(2, 0, 512, 0)
        ev_u(11, "s")
        ev_b(7, 1, "s")
        ev_u(10, "s")
        mm_o(0, 0, 512, 1)
        mm_o(3, 0, 512, 0)
        mm_o(1, 0, 512, 0, "tp")
        mm_o(1, 0, 512, 1)
        ev_b(6, 1, "s")
        quant_u(11)
        ev_o(0, 0, 512, "s")
        quant_b(0, 2)
        mm_o(3, 0, 512, 1)
        mm_u(8, [0, 1, 2, 3])
        ev_o(1, 0, 512, "s")
        quant_u(10)
        mm_o(3, 1280, 256, 0)
        inter_b(1, 1, "v")
        mm_o(1, 1280, 256, 0, "tp")
        mm_o(1, 1280, 256, 1)
        mm_o(0, 1280, 256, 0, "tp")
        ev_o(3, 0, 512, "s")
        mm_o(3, 1280, 256, 1)
        mm_o(2, 0, 512, 1)
        quant_b(0, 1)
        quant_b(1, 1)
        ev_u(8, "s")
        ev_o(1, 1280, 256, "s")
        mm_o(2, 1280, 256, 0)
        ev_o(3, 1280, 256, "s")
        mm_o(2, 1280, 256, 1)
        mm_o(0, 1280, 256, 1)
        ev_o(0, 1280, 256, "v")
        ev_o(2, 0, 512, "s")
        mm_u(9, [0, 1, 2, 3])
        quant_u(8)
        mm_o(0, 512, 512, 0, "tp")
        ev_o(2, 1280, 256, "s")
        mm_o(0, 512, 512, 1)
        ev_u(9, "v")
        mm_o(2, 512, 512, 0)
        ev_o(0, 512, 512, "s")
        mm_o(2, 512, 512, 1)
        quant_u(9)
        mm_o(1, 512, 512, 0, "tp")
        mm_o(1, 512, 512, 1)
        ev_o(2, 512, 512, "v")
        ev_o(1, 512, 512, "s")
        mm_o(3, 512, 512, 0)
        mm_o(3, 512, 512, 1)
        ev_o(3, 512, 512, "v")
        mm_o(0, 1024, 256, 0, "tp")
        mm_o(2, 1024, 256, 0)
        mm_o(3, 1024, 256, 0)
        mm_o(3, 1024, 256, 1)
        mm_o(0, 1024, 256, 1)
        mm_o(2, 1024, 256, 1)
        ev_o(3, 1024, 256, "v")
        mm_o(1, 1024, 256, 0, "tp")
        mm_o(1, 1024, 256, 1)
        ev_o(1, 1024, 256, "v")
        ev_o(2, 1024, 256, "s")
        ev_o(0, 1024, 256, "s")
